import numpy as np
import ml_dtypes


def mxq(x, axis, fmt="e4m3"):
    dtype, down = {"e4m3": (ml_dtypes.float8_e4m3fn, 7), "e5m2": (ml_dtypes.float8_e5m2, 14)}[fmt]
    v = np.moveaxis(np.asarray(x, np.float32).astype(ml_dtypes.bfloat16).astype(np.float64), axis, -1)
    blocks = v.reshape(v.shape[:-1] + (-1, 32))
    amax = np.abs(blocks).max(-1, keepdims=True)
    byte = np.maximum(np.where(amax > 0, np.frexp(amax)[1] - 1 + 127, 0) - down, 1)
    scale = np.exp2(byte - 127.0)
    codes = (blocks / scale).astype(np.float32).astype(dtype).astype(np.float64)
    return np.moveaxis((codes * scale).reshape(v.shape), -1, axis)


WIDE = False


def mx_kscale(k):
    if not WIDE:
        return np.ones(k)
    levels = np.array([10, -10, 5, -5, 0])
    if k % 512:
        return np.exp2(np.random.permutation(np.resize(levels, k // 32))).repeat(32)
    a = np.empty((k // 512, 16))
    for p in range(k // 512):
        a[p, :8] = np.random.permutation(np.resize(levels, 8))
        for g in range(8):
            far = levels[np.abs(levels - a[p, g]) >= 10]
            a[p, g + 8] = far[np.random.randint(len(far))]
    return np.exp2(a.ravel()).repeat(32)


def f64(x):
    return np.asarray(x).astype(np.float64)


def striped(idx):
    return np.tile(idx.reshape(-1, 16).T, (8, 1)).astype(np.uint16)


def unstriped(offs):
    return offs[:16].T.reshape(-1).astype(np.int64)


E2M1 = np.array([0.0, 0.5, 1.0, 1.5, 2.0, 3.0, 4.0, 6.0, -0.0, -0.5, -1.0, -1.5, -2.0, -3.0, -4.0, -6.0])


def pack_weight(w, fmt):
    k, n = w.shape
    w = f64(np.asarray(w, np.float32).astype(ml_dtypes.bfloat16)).reshape(k // 32, 32, n)
    amax = np.abs(w).max(1)
    if fmt == "e4m3":
        byte = np.frexp(amax)[1] - 1 + 127 - 7
    else:
        mant, ex = np.frexp(amax / 6.0)
        byte = np.where(mant > 0.5, ex, ex - 1) + 127
    byte = np.clip(np.where(amax > 0, byte, 1), 1, 254)
    scaled = (w * np.exp2(127.0 - byte)[:, None, :]).reshape(k, n).astype(np.float32)
    by_word = np.ascontiguousarray(scaled.reshape(k // 512, 128, 4, n).transpose(0, 1, 3, 2))
    if fmt == "e4m3":
        words = by_word.astype(ml_dtypes.float8_e4m3fn).view(np.uint8)
    else:
        c = by_word.astype(ml_dtypes.float4_e2m1fn).view(np.uint8) & 0xF
        words = (c[..., 0::2] | (c[..., 1::2] << 4)).reshape(k // 512, 128, 2 * n)
    return np.ascontiguousarray(words), np.ascontiguousarray(byte.astype(np.uint8).reshape(k // 512, 16, n))


def unpack_weight(words, scales, fmt):
    g, _, n = scales.shape
    words = np.ascontiguousarray(words).reshape(g, 128, n, -1)
    if fmt == "e4m3":
        vals = words.view(ml_dtypes.float8_e4m3fn).astype(np.float64)
    else:
        nib = np.empty((g, 128, n, 4), np.uint8)
        nib[..., 0::2] = words & 0xF
        nib[..., 1::2] = words >> 4
        vals = E2M1[nib]
    vals = vals * np.repeat(np.exp2(scales.astype(np.float64) - 127.0), 8, axis=1)[..., None]
    return vals.transpose(0, 1, 3, 2).reshape(g * 512, n)


def gelu(v):
    return 0.5 * v * (1.0 + np.tanh(np.sqrt(2.0 / np.pi) * (v + 0.044715 * v**3)))


K, H, N, T, S = 1024, 512, 1024, 2048, 1024

def setup_inputs():
    n = np.random.standard_normal
    s = mx_kscale(K)[:, None]
    u = mx_kscale(H)[:, None]
    tab_words, tab_scales = pack_weight(n((K, T)) * s, "e4m3")
    wg_words, wg_scales = pack_weight(1.5 * n((K, H)) / np.sqrt(K) / s, "e2m1")
    wo_words, wo_scales = pack_weight(n((K, H)) / np.sqrt(K) / s * u.T, "e4m3")
    return {
        "tab_words": tab_words, "tab_scales": tab_scales,
        "offs": striped(np.random.permutation(T)[:S]),
        "offs2": striped(np.random.permutation(T)[:S]),
        "offs3": striped(np.random.permutation(T)[:S]),
        "wg_words": wg_words, "wg_scales": wg_scales,
        "wp": (n((K, H)) / np.sqrt(K) / s * u.T).astype(np.float32),
        "wo_words": wo_words, "wo_scales": wo_scales,
        "we": (1.3 * n((H, N)) / np.sqrt(H) / u).astype(np.float32),
        "be": (0.5 * n(N)).astype(np.float32),
    }

def reference(tab_words, tab_scales, offs, offs2, offs3, wg_words, wg_scales, wp, wo_words, wo_scales, we, be):
    last = unpack_weight(tab_words, tab_scales, "e4m3")[:, unstriped(offs)]
    prev = unpack_weight(tab_words, tab_scales, "e4m3")[:, unstriped(offs2)]
    older = unpack_weight(tab_words, tab_scales, "e4m3")[:, unstriped(offs3)]
    wg = unpack_weight(wg_words, wg_scales, "e2m1")
    wo = unpack_weight(wo_words, wo_scales, "e4m3")
    z = wg.T @ last
    a = mxq(f64(wp), 0, "e4m3").T @ prev
    b = wo.T @ older
    g = 1.0 / (1.0 + np.exp(-z))
    h = b + g * (a - b)
    y = mxq(f64(we), 0, "e4m3").T @ mxq(h, 0, "e4m3")
    return y + f64(be)[:, None]

@@ -1,0 +1,280 @@
+from contextlib import ExitStack
+
+import concourse.mybir as mybir
+from concourse.masks import make_identity
+
+K, H, N, T, S = 1024, 512, 1024, 2048, 1024
+FLOPS = 2 * (3 * K * H * S + H * N * S)
+
+F32 = mybir.dt.float32
+BF16 = mybir.dt.bfloat16
+I32 = mybir.dt.int32
+U32 = mybir.dt.uint32
+U16 = mybir.dt.uint16
+U8 = mybir.dt.uint8
+FP8X4 = mybir.dt.float8_e4m3fn_x4
+FP4X4 = mybir.dt.float4_e2m1fn_x4
+ACT = mybir.ActivationFunctionType
+ALU = mybir.AluOpType
+
+P = 128
+PACK = 4
+PASSES = K // (P * PACK)
+QUADS = 4
+CHUNK = 256
+CHUNKS = S // CHUNK
+UNIT = 128
+UNITS = S // UNIT
+ZB = 1
+AB = 2
+BB = 2
+HB = 1
+YB = 2
+TL = 0
+LAG = 3
+WE_STEP = 1
+VC = 3
+N_TILES = N // P
+HALF = N // 2
+
+
+def tile_list_session_gate_scores_kernel(
+    tc, tab_words, tab_scales, offs, offs2, offs3, wg_words, wg_scales, wp, wo_words, wo_scales, we, be, out
+):
+    nc = tc.nc
+    with ExitStack() as ctx:
+        keep = ctx.enter_context(tc.tile_pool(name="keep", bufs=1))
+        ring = ctx.enter_context(tc.tile_pool(name="ring", bufs=2))
+        psum = ctx.enter_context(tc.psum_pool(name="psum", bufs=1))
+
+        lists = [keep.tile([P, S // 16], U16, name=f"list{i}") for i in range(3)]
+        tab_s = keep.tile([P, T], U8, align_bytes=64)
+        tab_w = [keep.tile([P, T], I32, name=f"tab_w{a}", align_bytes=64) for a in range(PASSES)]
+        wg_w = keep.tile([P, PASSES, 2 * H], U8, align_bytes=64)
+        wg_s = keep.tile([P, PASSES, H], U8, align_bytes=64)
+        wo_w = keep.tile([P, PASSES, H], I32, align_bytes=64)
+        wo_s = keep.tile([P, H], U8, align_bytes=64)
+        last_s1 = keep.tile([P, S], U8, align_bytes=64)
+        bias = keep.tile([P, N_TILES], F32)
+        ident = keep.tile([P, P], F32)
+        warm = keep.tile([P, 2], F32)
+
+        nc.vector.memset(tab_s[:].bitcast(I32), 0)
+        nc.vector.memset(wo_s[:].bitcast(I32), 0)
+        nc.vector.memset(last_s1[:].bitcast(I32), 0)
+        nc.vector.memset(warm[:, 0:1], 0.0)
+        nc.scalar.activation(warm[:, 1:2], warm[:, 0:1], ACT.Sigmoid)
+        nc.gpsimd.memset(wg_s[:].bitcast(I32), 0)
+        for q in range(QUADS):
+            nc.gpsimd.dma_start(
+                wg_s[32 * q : 32 * q + 4, :, :].bitcast(I32),
+                wg_scales[:, 4 * q : 4 * q + 4, :].rearrange("a r c -> r a c").bitcast(I32),
+            )
+        for q in range(QUADS):
+            nc.gpsimd.dma_start(
+                wo_s[32 * q : 32 * q + 8, :].bitcast(I32), wo_scales[:, 4 * q : 4 * q + 4, :].bitcast(I32)
+            )
+        make_identity(nc, ident[:])
+
+        nc.sync.dma_start(lists[0][:], offs)
+        for q in range(QUADS):
+            nc.sync.dma_start(
+                tab_s[32 * q : 32 * q + 8, :].bitcast(I32), tab_scales[:, 4 * q : 4 * q + 4, :].bitcast(I32)
+            )
+
+        got_s = [keep.tile([P, S], U8, name=f"got_s{i}", align_bytes=64) for i in range(3)]
+        nc.vector.tensor_copy(got_s[0][:], tab_s[:].indirect(lists[0][:]))
+
+        def load_rows(rows, name):
+            raw = keep.tile([P, PACK, HALF], F32, name=name)
+            nc.sync.dma_start(raw[:], rows.rearrange("(p j) w -> p j w", j=PACK))
+            return raw
+
+        def quantise(raw, name, pieces):
+            grouped = keep.tile([P, HALF, PACK], BF16, name=name + "_b", tag=name + "_b", align_bytes=64)
+            for k in range(pieces):
+                part = slice(k * HALF // pieces, (k + 1) * HALF // pieces)
+                nc.scalar.copy(
+                    grouped[:, part, :].rearrange("p (c i) t -> p c t i", i=4),
+                    raw[:, :, part].rearrange("p t (c i) -> p c t i", i=4),
+                )
+            codes = keep.tile([P, HALF], U32, name=name + "_w", align_bytes=64)
+            scales = keep.tile([P, HALF], U8, name=name + "_s", align_bytes=64)
+            nc.vector.quantize_mx(codes[:].bitcast(FP8X4), scales[:], grouped[:].rearrange("p c t -> p (c t)"))
+            return codes, scales
+
+        def load_table(a):
+            nc.sync.dma_start(tab_w[a][:], tab_words[a].rearrange("p t i -> p (t i)").bitcast(I32))
+
+        wp_raw = [load_rows(wp[0:512, :], "wp0")]
+        nc.sync.dma_start(lists[1][:], offs2)
+        nc.sync.dma_start(lists[2][:], offs3)
+        for i in (1, 2):
+            nc.vector.tensor_copy(got_s[i][:], tab_s[:].indirect(lists[i][:]))
+        wp_raw.append(load_rows(wp[512:1024, :], "wp1"))
+        load_table(0)
+        for q in range(QUADS):
+            nc.scalar.dma_start(
+                last_s1[32 * q : 32 * q + 4, :].bitcast(I32), got_s[0][32 * q + 4 : 32 * q + 8, :].bitcast(I32)
+            )
+        load_table(1)
+        nc.sync.dma_start(wg_w[:].bitcast(I32), wg_words.rearrange("a p c -> p a c").bitcast(I32))
+        nc.sync.dma_start(wo_w[:], wo_words.rearrange("a p c i -> p a (c i)").bitcast(I32))
+        we_raw = [load_rows(we[:, h * HALF : (h + 1) * HALF], f"we{h}") for h in range(2)]
+        with nc.allow_non_contiguous_dma(reason="one bias value a partition and output tile"):
+            nc.sync.dma_start(bias[:], be.rearrange("(t p) -> p t", p=P))
+
+        wp_q = [quantise(wp_raw[a], f"wp{a}", 1) for a in range(PASSES)]
+        we_q = []
+
+        out_v = out.rearrange("(t p) j -> p t j", p=P)
+        got = {}
+
+        def gather(i, c, a, dest):
+            got[i, c, a] = dest
+            cols = slice(c * CHUNK // 16, (c + 1) * CHUNK // 16)
+            nc.vector.tensor_copy(dest, tab_w[a][:].bitcast(U32).indirect(lists[i][:, cols]))
+
+        def gather_into(tag, wanted):
+            wanted = [(i, c) for i, c in wanted if c < CHUNKS]
+            if wanted:
+                dest = keep.tile([P, len(wanted), PASSES, CHUNK], U32, name="got_" + tag, tag=tag, align_bytes=64)
+                for k, (i, c) in enumerate(wanted):
+                    for a in range(PASSES):
+                        gather(i, c, a, dest[:, k, a, :])
+
+        first = keep.tile([P, PASSES, 3, CHUNK], U32, align_bytes=64)
+        for a in range(PASSES):
+            for i in range(3):
+                gather(i, 0, a, first[:, a, i, :])
+        gather_into("wp1_b", [(0, 1)])
+
+        dealt = "j (p t) -> j t p"
+        sums = {}
+        terms = {}
+        states = {}
+        packed = {}
+
+        gates = {}
+
+        def gate_of(u):
+            c, v = divmod(u, 2)
+            loc = slice(v * UNIT, (v + 1) * UNIT)
+            glob = slice(u * UNIT, (u + 1) * UNIT)
+            z_ps = psum.tile([P, H], F32, bufs=ZB)
+            for a in range(PASSES):
+                nc.tensor.matmul_mx(
+                    z_ps[:],
+                    lhsT=got[0, c, a][:, loc].bitcast(FP8X4),
+                    lhsT_scale=(got_s[0] if a == 0 else last_s1)[:, glob],
+                    rhs=wg_w[:, a, :].bitcast(FP4X4),
+                    rhs_scale=wg_s[:, a, :],
+                    start=(a == 0),
+                    stop=(a == PASSES - 1),
+                )
+            gate = keep.tile([P, PACK, P], F32, name="gate", tag=f"gate{u}", align_bytes=64)
+            nc.scalar.activation(gate[:], z_ps[:].rearrange(dealt, t=PACK), ACT.Sigmoid)
+            gates[u] = gate
+
+        def products(u):
+            c, v = divmod(u, 2)
+            loc = slice(v * UNIT, (v + 1) * UNIT)
+            glob = slice(u * UNIT, (u + 1) * UNIT)
+            a_ps = psum.tile([P, H], F32, bufs=AB)
+            b_ps = psum.tile([P, H], F32, bufs=BB)
+            for a in range(PASSES):
+                nc.tensor.matmul_mx(
+                    a_ps[:],
+                    lhsT=got[1, c, a][:, loc].bitcast(FP8X4),
+                    lhsT_scale=got_s[1][4 * a :, glob],
+                    rhs=wp_q[a][0][:].bitcast(FP8X4),
+                    rhs_scale=wp_q[a][1][:],
+                    start=(a == 0),
+                    stop=(a == PASSES - 1),
+                )
+            for a in range(PASSES):
+                nc.tensor.matmul_mx(
+                    b_ps[:],
+                    lhsT=got[2, c, a][:, loc].bitcast(FP8X4),
+                    lhsT_scale=got_s[2][4 * a :, glob],
+                    rhs=wo_w[:, a, :].bitcast(FP8X4),
+                    rhs_scale=wo_s[4 * a :, :],
+                    start=(a == 0),
+                    stop=(a == PASSES - 1),
+                )
+            sums[u] = (gates[u], a_ps, b_ps)
+
+        def gated_terms(u):
+            c, v = divmod(u, 2)
+            gate, a_ps, b_ps = sums[u]
+            neg_ga = ring.tile([P, PACK, P], F32, bufs=3)
+            nc.vector.scalar_tensor_tensor(
+                neg_ga[:], gate[:], -1.0, a_ps[:].rearrange(dealt, t=PACK), ALU.mult, ALU.mult
+            )
+            neg_rest = ring.tile([P, PACK, P], F32, bufs=3)
+            nc.vector.scalar_tensor_tensor(
+                neg_rest[:], gate[:], 1.0, b_ps[:].rearrange(dealt, t=PACK), ALU.subtract, ALU.mult
+            )
+            terms[u] = (neg_ga, neg_rest)
+            gather_into(f"gate{u}", [(1, c + 1)] if v == 0 else [(2, c + 1), (0, c + 2)])
+
+        def turn(u):
+            c, v = divmod(u, 2)
+            neg_ga, neg_rest = terms[u]
+            if v == 0:
+                states[c] = ring.tile([P, CHUNK, PACK], BF16, name="state", align_bytes=64)
+            h_ps = psum.tile([P, PACK, UNIT], F32, bufs=HB)
+            for t in range(PACK):
+                nc.tensor.matmul(h_ps[:, t, :], neg_rest[:, t, :], ident[:], start=True, stop=False, is_transpose=True)
+                nc.tensor.matmul(h_ps[:, t, :], neg_ga[:, t, :], ident[:], start=False, stop=True, is_transpose=True)
+            nc.scalar.activation(
+                states[c][:, v * UNIT : (v + 1) * UNIT, :], h_ps[:].rearrange("p t j -> p j t"), ACT.Copy, scale=-1.0
+            )
+            if v == 1:
+                h_w = ring.tile([P, CHUNK], U32, align_bytes=64)
+                h_s = ring.tile([P, CHUNK], U8, align_bytes=64)
+                nc.vector.quantize_mx(h_w[:].bitcast(FP8X4), h_s[:], states[c][:].rearrange("p j t -> p (j t)"))
+                packed[c] = (h_w, h_s)
+
+        def scores(c, pair):
+            h_w, h_s = packed[c]
+            y_ps = psum.tile([P, 2, CHUNK], F32, bufs=YB)
+            y_sb = ring.tile([P, 2, CHUNK], F32, bufs=6)
+            for e in range(2):
+                nt = 2 * pair + e
+                codes, scales = we_q[nt * P // HALF]
+                ncols = slice(nt * P % HALF, nt * P % HALF + P)
+                nc.tensor.matmul_mx(
+                    y_ps[:, e, :],
+                    lhsT=codes[:, ncols].bitcast(FP8X4),
+                    lhsT_scale=scales[:, ncols],
+                    rhs=h_w[:].bitcast(FP8X4),
+                    rhs_scale=h_s[:],
+                    start=True,
+                    stop=True,
+                )
+            on_vector = c >= VC and pair % 2 == 1
+            for e in range(2):
+                nt = 2 * pair + e
+                if on_vector:
+                    nc.vector.tensor_scalar_add(y_sb[:, e, :], y_ps[:, e, :], bias[:, nt : nt + 1])
+                else:
+                    nc.scalar.activation(y_sb[:, e, :], y_ps[:, e, :], ACT.Identity, bias=bias[:, nt : nt + 1])
+            nc.sync.dma_start(out_v[:, 2 * pair : 2 * pair + 2, c * CHUNK : (c + 1) * CHUNK], y_sb[:])
+
+        gate_of(0)
+        for step in range(UNITS + LAG + 2):
+            if step < UNITS:
+                products(step)
+            if step + 1 < UNITS:
+                gate_of(step + 1)
+            if step < UNITS:
+                gated_terms(step)
+            if TL <= step < UNITS + TL:
+                turn(step - TL)
+            if step == WE_STEP:
+                we_q.extend(quantise(we_raw[h], f"we{h}", 4) for h in range(2))
+            done = step - LAG
+            if done >= 0 and done // 2 < CHUNKS:
+                for pair in range(2):
+                    scores(done // 2, 2 * (done % 2) + pair)

@@ -30,10 +30,9 @@ AB = 2
 BB = 2
 HB = 1
 YB = 2
-TL = 0
-LAG = 3
-WE_STEP = 1
+LAG = 2
 VC = 3
+WH = 0
 N_TILES = N // P
 HALF = N // 2
 
@@ -48,7 +47,7 @@ def tile_list_session_gate_scores_kernel(
         psum = ctx.enter_context(tc.psum_pool(name="psum", bufs=1))
 
         lists = [keep.tile([P, S // 16], U16, name=f"list{i}") for i in range(3)]
-        tab_s = keep.tile([P, T], U8, align_bytes=64)
+        tab_s = keep.tile([P, T], U8, tag="tab_s", align_bytes=64)
         tab_w = [keep.tile([P, T], I32, name=f"tab_w{a}", align_bytes=64) for a in range(PASSES)]
         wg_w = keep.tile([P, PASSES, 2 * H], U8, align_bytes=64)
         wg_s = keep.tile([P, PASSES, H], U8, align_bytes=64)
@@ -60,11 +59,12 @@ def tile_list_session_gate_scores_kernel(
         warm = keep.tile([P, 2], F32)
 
         nc.vector.memset(tab_s[:].bitcast(I32), 0)
+        nc.vector.memset(wg_s[:].bitcast(I32), 0)
         nc.vector.memset(wo_s[:].bitcast(I32), 0)
         nc.vector.memset(last_s1[:].bitcast(I32), 0)
         nc.vector.memset(warm[:, 0:1], 0.0)
+        nc.vector.memset(ident[:], 0.0)
         nc.scalar.activation(warm[:, 1:2], warm[:, 0:1], ACT.Sigmoid)
-        nc.gpsimd.memset(wg_s[:].bitcast(I32), 0)
         for q in range(QUADS):
             nc.gpsimd.dma_start(
                 wg_s[32 * q : 32 * q + 4, :, :].bitcast(I32),
@@ -74,7 +74,9 @@ def tile_list_session_gate_scores_kernel(
             nc.gpsimd.dma_start(
                 wo_s[32 * q : 32 * q + 8, :].bitcast(I32), wo_scales[:, 4 * q : 4 * q + 4, :].bitcast(I32)
             )
-        make_identity(nc, ident[:])
+        with nc.allow_non_contiguous_dma(reason="one bias value a partition and output tile"):
+            nc.gpsimd.dma_start(bias[:], be.rearrange("(t p) -> p t", p=P))
+        make_identity(nc, ident[:], nomemset=True)
 
         nc.sync.dma_start(lists[0][:], offs)
         for q in range(QUADS):
@@ -85,20 +87,25 @@ def tile_list_session_gate_scores_kernel(
         got_s = [keep.tile([P, S], U8, name=f"got_s{i}", align_bytes=64) for i in range(3)]
         nc.vector.tensor_copy(got_s[0][:], tab_s[:].indirect(lists[0][:]))
 
-        def load_rows(rows, name):
-            raw = keep.tile([P, PACK, HALF], F32, name=name)
+        def load_rows(rows, name, tag):
+            raw = keep.tile([P, PACK, HALF], F32, name=name, tag=tag, align_bytes=64)
             nc.sync.dma_start(raw[:], rows.rearrange("(p j) w -> p j w", j=PACK))
             return raw
 
-        def quantise(raw, name, pieces):
+        def quantise(raw, name, pieces, on_gpsimd, tag):
             grouped = keep.tile([P, HALF, PACK], BF16, name=name + "_b", tag=name + "_b", align_bytes=64)
             for k in range(pieces):
                 part = slice(k * HALF // pieces, (k + 1) * HALF // pieces)
-                nc.scalar.copy(
-                    grouped[:, part, :].rearrange("p (c i) t -> p c t i", i=4),
-                    raw[:, :, part].rearrange("p t (c i) -> p c t i", i=4),
-                )
-            codes = keep.tile([P, HALF], U32, name=name + "_w", align_bytes=64)
+                if on_gpsimd:
+                    nc.gpsimd.tensor_scalar(
+                        grouped[:, part, :], raw[:, :, part].rearrange("p t c -> p c t"), 1.0, 0.0, ALU.mult, ALU.add
+                    )
+                else:
+                    nc.scalar.copy(
+                        grouped[:, part, :].rearrange("p (c i) t -> p c t i", i=4),
+                        raw[:, :, part].rearrange("p t (c i) -> p c t i", i=4),
+                    )
+            codes = keep.tile([P, HALF], U32, name=name + "_w", tag=tag, align_bytes=64)
             scales = keep.tile([P, HALF], U8, name=name + "_s", align_bytes=64)
             nc.vector.quantize_mx(codes[:].bitcast(FP8X4), scales[:], grouped[:].rearrange("p c t -> p (c t)"))
             return codes, scales
@@ -106,25 +113,25 @@ def tile_list_session_gate_scores_kernel(
         def load_table(a):
             nc.sync.dma_start(tab_w[a][:], tab_words[a].rearrange("p t i -> p (t i)").bitcast(I32))
 
-        wp_raw = [load_rows(wp[0:512, :], "wp0")]
         nc.sync.dma_start(lists[1][:], offs2)
         nc.sync.dma_start(lists[2][:], offs3)
+        wp_raw = [load_rows(wp[0:512, :], "wp0", "wp0")]
         for i in (1, 2):
             nc.vector.tensor_copy(got_s[i][:], tab_s[:].indirect(lists[i][:]))
-        wp_raw.append(load_rows(wp[512:1024, :], "wp1"))
         load_table(0)
+        nc.sync.dma_start(wg_w[:].bitcast(I32), wg_words.rearrange("a p c -> p a c").bitcast(I32))
+        wp_raw.append(load_rows(wp[512:1024, :], "wp1", "wp1"))
         for q in range(QUADS):
             nc.scalar.dma_start(
                 last_s1[32 * q : 32 * q + 4, :].bitcast(I32), got_s[0][32 * q + 4 : 32 * q + 8, :].bitcast(I32)
             )
         load_table(1)
-        nc.sync.dma_start(wg_w[:].bitcast(I32), wg_words.rearrange("a p c -> p a c").bitcast(I32))
         nc.sync.dma_start(wo_w[:], wo_words.rearrange("a p c i -> p a (c i)").bitcast(I32))
-        we_raw = [load_rows(we[:, h * HALF : (h + 1) * HALF], f"we{h}") for h in range(2)]
-        with nc.allow_non_contiguous_dma(reason="one bias value a partition and output tile"):
-            nc.sync.dma_start(bias[:], be.rearrange("(t p) -> p t", p=P))
+        wp_q = [quantise(wp_raw[a], f"wp{a}", 1, False, f"wp{a}_w") for a in range(PASSES)]
+        we_raw = [
+            load_rows(we[:, h * HALF : (h + 1) * HALF], f"we{h}", tag) for h, tag in enumerate(("tab_s", "wp0"))
+        ]
 
-        wp_q = [quantise(wp_raw[a], f"wp{a}", 1) for a in range(PASSES)]
         we_q = []
 
         out_v = out.rearrange("(t p) j -> p t j", p=P)
@@ -143,11 +150,10 @@ def tile_list_session_gate_scores_kernel(
                     for a in range(PASSES):
                         gather(i, c, a, dest[:, k, a, :])
 
-        first = keep.tile([P, PASSES, 3, CHUNK], U32, align_bytes=64)
+        first = keep.tile([P, PASSES, 5, CHUNK], U32, align_bytes=64)
         for a in range(PASSES):
-            for i in range(3):
-                gather(i, 0, a, first[:, a, i, :])
-        gather_into("wp1_b", [(0, 1)])
+            for k, (i, c) in enumerate([(0, 0), (1, 0), (2, 0), (0, 1), (1, 1)]):
+                gather(i, c, a, first[:, a, k, :])
 
         dealt = "j (p t) -> j t p"
         sums = {}
@@ -202,12 +208,13 @@ def tile_list_session_gate_scores_kernel(
                     start=(a == 0),
                     stop=(a == PASSES - 1),
                 )
-            sums[u] = (gates[u], a_ps, b_ps)
+            sums[u] = (a_ps, b_ps)
 
         def gated_terms(u):
             c, v = divmod(u, 2)
-            gate, a_ps, b_ps = sums[u]
-            neg_ga = ring.tile([P, PACK, P], F32, bufs=3)
+            gate = gates[u]
+            a_ps, b_ps = sums[u]
+            neg_ga = keep.tile([P, PACK, P], F32, name="neg_ga", tag=f"neg_ga{u}", align_bytes=64)
             nc.vector.scalar_tensor_tensor(
                 neg_ga[:], gate[:], -1.0, a_ps[:].rearrange(dealt, t=PACK), ALU.mult, ALU.mult
             )
@@ -216,7 +223,7 @@ def tile_list_session_gate_scores_kernel(
                 neg_rest[:], gate[:], 1.0, b_ps[:].rearrange(dealt, t=PACK), ALU.subtract, ALU.mult
             )
             terms[u] = (neg_ga, neg_rest)
-            gather_into(f"gate{u}", [(1, c + 1)] if v == 0 else [(2, c + 1), (0, c + 2)])
+            gather_into(f"gate{u}", [(2, c + 1)] if v == 0 else [(0, c + 2), (1, c + 2)])
 
         def turn(u):
             c, v = divmod(u, 2)
@@ -262,19 +269,22 @@ def tile_list_session_gate_scores_kernel(
                     nc.scalar.activation(y_sb[:, e, :], y_ps[:, e, :], ACT.Identity, bias=bias[:, nt : nt + 1])
             nc.sync.dma_start(out_v[:, 2 * pair : 2 * pair + 2, c * CHUNK : (c + 1) * CHUNK], y_sb[:])
 
-        gate_of(0)
+        for u in range(2):
+            gate_of(u)
+            products(u)
+        gated_terms(0)
         for step in range(UNITS + LAG + 2):
-            if step < UNITS:
-                products(step)
+            if step + 2 < UNITS:
+                gate_of(step + 2)
             if step + 1 < UNITS:
-                gate_of(step + 1)
+                gated_terms(step + 1)
             if step < UNITS:
-                gated_terms(step)
-            if TL <= step < UNITS + TL:
-                turn(step - TL)
-            if step == WE_STEP:
-                we_q.extend(quantise(we_raw[h], f"we{h}", 4) for h in range(2))
+                turn(step)
+            if step + 2 < UNITS:
+                products(step + 2)
             done = step - LAG
+            if 0 <= done < 2:
+                we_q.append(quantise(we_raw[done], f"we{done}", 4, False, f"neg_ga{done + WH}"))
             if done >= 0 and done // 2 < CHUNKS:
                 for pair in range(2):
                     scores(done // 2, 2 * (done % 2) + pair)

@@ -26,13 +26,22 @@ CHUNKS = S // CHUNK
 UNIT = 128
 UNITS = S // UNIT
 ZB = 1
-AB = 2
-BB = 2
+AB = 1
+BB = 1
 HB = 1
-YB = 2
+YB = 4
+AHEAD = 1
+PF = 1
+SP = 1
 LAG = 2
-VC = 3
-WH = 0
+PER_STEP = 2
+FINE = 3
+VS = 6
+BANK = 512
+HOLD = {}
+FIRST = [(0, 1)]
+EVEN = [(1, 1)]
+ODD = [(2, 1), (0, 2)]
 N_TILES = N // P
 HALF = N // 2
 
@@ -74,8 +83,6 @@ def tile_list_session_gate_scores_kernel(
             nc.gpsimd.dma_start(
                 wo_s[32 * q : 32 * q + 8, :].bitcast(I32), wo_scales[:, 4 * q : 4 * q + 4, :].bitcast(I32)
             )
-        with nc.allow_non_contiguous_dma(reason="one bias value a partition and output tile"):
-            nc.gpsimd.dma_start(bias[:], be.rearrange("(t p) -> p t", p=P))
         make_identity(nc, ident[:], nomemset=True)
 
         nc.sync.dma_start(lists[0][:], offs)
@@ -92,13 +99,23 @@ def tile_list_session_gate_scores_kernel(
             nc.sync.dma_start(raw[:], rows.rearrange("(p j) w -> p j w", j=PACK))
             return raw
 
-        def quantise(raw, name, pieces, on_gpsimd, tag):
+        def load_dealt(rows, name, tag):
+            raw = keep.tile([P, PACK, HALF], F32, name=name, tag=tag, align_bytes=64)
+            by_slot = rows.rearrange("(q t i) w -> t q i w", t=PACK, i=8)
+            for t in range(PACK):
+                nc.sync.dma_start(raw[:, t, :], by_slot[t])
+            return raw
+
+        def quantise(raw, name, pieces, dealt, tag):
             grouped = keep.tile([P, HALF, PACK], BF16, name=name + "_b", tag=name + "_b", align_bytes=64)
             for k in range(pieces):
                 part = slice(k * HALF // pieces, (k + 1) * HALF // pieces)
-                if on_gpsimd:
-                    nc.gpsimd.tensor_scalar(
-                        grouped[:, part, :], raw[:, :, part].rearrange("p t c -> p c t"), 1.0, 0.0, ALU.mult, ALU.add
+                if dealt:
+                    nc.scalar.activation(
+                        grouped[:, part, :].rearrange("p (q i) j -> p q i j", i=8),
+                        raw[:].rearrange("p j (q t i) -> p t q i j", t=PACK, i=8)[:, k],
+                        ACT.Copy,
+                        scale=-1.0,
                     )
                 else:
                     nc.scalar.copy(
@@ -127,13 +144,15 @@ def tile_list_session_gate_scores_kernel(
             )
         load_table(1)
         nc.sync.dma_start(wo_w[:], wo_words.rearrange("a p c i -> p a (c i)").bitcast(I32))
-        wp_q = [quantise(wp_raw[a], f"wp{a}", 1, False, f"wp{a}_w") for a in range(PASSES)]
+        wp_q = [quantise(wp_raw[a], f"wp{a}", PACK, True, f"wp{a}_w") for a in range(PASSES)]
         we_raw = [
-            load_rows(we[:, h * HALF : (h + 1) * HALF], f"we{h}", tag) for h, tag in enumerate(("tab_s", "wp0"))
+            load_dealt(we[:, h * HALF : (h + 1) * HALF], f"we{h}", tag) for h, tag in enumerate(("tab_s", "wp0"))
         ]
 
         we_q = []
 
+        with nc.allow_non_contiguous_dma(reason="one bias value a partition and output tile"):
+            nc.sync.dma_start(bias[:], be.rearrange("(t p) -> p t", p=P))
         out_v = out.rearrange("(t p) j -> p t j", p=P)
         got = {}
 
@@ -150,16 +169,18 @@ def tile_list_session_gate_scores_kernel(
                     for a in range(PASSES):
                         gather(i, c, a, dest[:, k, a, :])
 
-        first = keep.tile([P, PASSES, 5, CHUNK], U32, align_bytes=64)
+        first = keep.tile([P, PASSES, 3, CHUNK], U32, align_bytes=64)
         for a in range(PASSES):
-            for k, (i, c) in enumerate([(0, 0), (1, 0), (2, 0), (0, 1), (1, 1)]):
-                gather(i, c, a, first[:, a, k, :])
+            for i in range(3):
+                gather(i, 0, a, first[:, a, i, :])
+        gather_into("wp1_b", FIRST)
 
-        dealt = "j (p t) -> j t p"
+        dealt = "j (q t i) -> j t q i"
+        by_block = "j t (q i) -> j t q i"
         sums = {}
         terms = {}
         states = {}
-        packed = {}
+        waiting = []
 
         gates = {}
 
@@ -179,7 +200,9 @@ def tile_list_session_gate_scores_kernel(
                     stop=(a == PASSES - 1),
                 )
             gate = keep.tile([P, PACK, P], F32, name="gate", tag=f"gate{u}", align_bytes=64)
-            nc.scalar.activation(gate[:], z_ps[:].rearrange(dealt, t=PACK), ACT.Sigmoid)
+            nc.scalar.activation(
+                gate[:].rearrange(by_block, i=8), z_ps[:].rearrange(dealt, t=PACK, i=8), ACT.Sigmoid, scale=-1.0
+            )
             gates[u] = gate
 
         def products(u):
@@ -214,41 +237,51 @@ def tile_list_session_gate_scores_kernel(
             c, v = divmod(u, 2)
             gate = gates[u]
             a_ps, b_ps = sums[u]
-            neg_ga = keep.tile([P, PACK, P], F32, name="neg_ga", tag=f"neg_ga{u}", align_bytes=64)
+            both = keep.tile([P, 2, PACK, P], F32, name="terms", tag=HOLD.get(u, f"terms{u}"), align_bytes=64)
+            neg_ga = both[:, 0]
+            neg_rest = both[:, 1]
             nc.vector.scalar_tensor_tensor(
-                neg_ga[:], gate[:], -1.0, a_ps[:].rearrange(dealt, t=PACK), ALU.mult, ALU.mult
+                neg_ga[:], gate[:], 1.0, a_ps[:].rearrange("j (t p) -> j t p", t=PACK), ALU.subtract, ALU.mult
             )
-            neg_rest = ring.tile([P, PACK, P], F32, bufs=3)
-            nc.vector.scalar_tensor_tensor(
-                neg_rest[:], gate[:], 1.0, b_ps[:].rearrange(dealt, t=PACK), ALU.subtract, ALU.mult
+            nc.vector.tensor_tensor(
+                neg_rest[:].rearrange(by_block, i=8),
+                gate[:].rearrange(by_block, i=8),
+                b_ps[:].rearrange(dealt, t=PACK, i=8),
+                ALU.mult,
             )
             terms[u] = (neg_ga, neg_rest)
-            gather_into(f"gate{u}", [(2, c + 1)] if v == 0 else [(0, c + 2), (1, c + 2)])
+            gather_into(f"gate{u}", [(i, c + k) for i, k in (EVEN if v == 0 else ODD)])
 
         def turn(u):
             c, v = divmod(u, 2)
             neg_ga, neg_rest = terms[u]
             if v == 0:
-                states[c] = ring.tile([P, CHUNK, PACK], BF16, name="state", align_bytes=64)
+                states[c] = keep.tile([P, CHUNK, PACK], BF16, name="state", tag=f"state{c}", align_bytes=64)
             h_ps = psum.tile([P, PACK, UNIT], F32, bufs=HB)
             for t in range(PACK):
                 nc.tensor.matmul(h_ps[:, t, :], neg_rest[:, t, :], ident[:], start=True, stop=False, is_transpose=True)
                 nc.tensor.matmul(h_ps[:, t, :], neg_ga[:, t, :], ident[:], start=False, stop=True, is_transpose=True)
-            nc.scalar.activation(
-                states[c][:, v * UNIT : (v + 1) * UNIT, :], h_ps[:].rearrange("p t j -> p j t"), ACT.Copy, scale=-1.0
-            )
-            if v == 1:
-                h_w = ring.tile([P, CHUNK], U32, align_bytes=64)
-                h_s = ring.tile([P, CHUNK], U8, align_bytes=64)
-                nc.vector.quantize_mx(h_w[:].bitcast(FP8X4), h_s[:], states[c][:].rearrange("p j t -> p (j t)"))
-                packed[c] = (h_w, h_s)
+            nc.scalar.copy(states[c][:, v * UNIT : (v + 1) * UNIT, :], h_ps[:].rearrange("p t j -> p j t"))
+            if c >= FINE:
+                pack(u * UNIT, UNIT, states[c][:, v * UNIT : (v + 1) * UNIT, :])
+            elif v == 1:
+                pack(c * CHUNK, CHUNK, states[c][:])
 
-        def scores(c, pair):
-            h_w, h_s = packed[c]
-            y_ps = psum.tile([P, 2, CHUNK], F32, bufs=YB)
-            y_sb = ring.tile([P, 2, CHUNK], F32, bufs=6)
-            for e in range(2):
-                nt = 2 * pair + e
+        def pack(j0, width, values):
+            h_w = keep.tile([P, width], U32, name=f"h_w{j0}", align_bytes=64)
+            h_s = keep.tile([P, width], U8, name=f"h_s{j0}", align_bytes=64)
+            nc.vector.quantize_mx(h_w[:].bitcast(FP8X4), h_s[:], values.rearrange("p j t -> p (j t)"))
+            per_bank = BANK // width
+            for first_tile in range(0, N_TILES, per_bank):
+                waiting.append((h_w, h_s, j0, width, first_tile))
+
+        def scores(on_vector):
+            h_w, h_s, j0, width, first_tile = waiting.pop(0)
+            per_bank = BANK // width
+            y_ps = psum.tile([P, per_bank, width], F32, bufs=YB)
+            y_sb = ring.tile([P, per_bank, width], F32, bufs=8)
+            for e in range(per_bank):
+                nt = first_tile + e
                 codes, scales = we_q[nt * P // HALF]
                 ncols = slice(nt * P % HALF, nt * P % HALF + P)
                 nc.tensor.matmul_mx(
@@ -260,31 +293,37 @@ def tile_list_session_gate_scores_kernel(
                     start=True,
                     stop=True,
                 )
-            on_vector = c >= VC and pair % 2 == 1
-            for e in range(2):
-                nt = 2 * pair + e
+            for e in range(per_bank):
+                nt = first_tile + e
                 if on_vector:
                     nc.vector.tensor_scalar_add(y_sb[:, e, :], y_ps[:, e, :], bias[:, nt : nt + 1])
                 else:
                     nc.scalar.activation(y_sb[:, e, :], y_ps[:, e, :], ACT.Identity, bias=bias[:, nt : nt + 1])
-            nc.sync.dma_start(out_v[:, 2 * pair : 2 * pair + 2, c * CHUNK : (c + 1) * CHUNK], y_sb[:])
+            nc.sync.dma_start(out_v[:, first_tile : first_tile + per_bank, j0 : j0 + width], y_sb[:])
 
-        for u in range(2):
-            gate_of(u)
+        def some_scores(step):
+            if step >= LAG:
+                for k in range(min(PER_STEP if step < UNITS else len(waiting), len(waiting))):
+                    scores(step >= VS and k % 2 == 1)
+
+        gate_of(0)
+        for u in range(AHEAD):
             products(u)
-        gated_terms(0)
-        for step in range(UNITS + LAG + 2):
-            if step + 2 < UNITS:
-                gate_of(step + 2)
-            if step + 1 < UNITS:
-                gated_terms(step + 1)
+        gate_of(1)
+        for step in range(UNITS + 1):
+            if step < UNITS:
+                gated_terms(step)
+            if PF and step + AHEAD < UNITS:
+                products(step + AHEAD)
+            if SP == 0:
+                some_scores(step)
             if step < UNITS:
                 turn(step)
             if step + 2 < UNITS:
-                products(step + 2)
-            done = step - LAG
-            if 0 <= done < 2:
-                we_q.append(quantise(we_raw[done], f"we{done}", 4, False, f"neg_ga{done + WH}"))
-            if done >= 0 and done // 2 < CHUNKS:
-                for pair in range(2):
-                    scores(done // 2, 2 * (done % 2) + pair)
+                gate_of(step + 2)
+            if not PF and step + AHEAD < UNITS:
+                products(step + AHEAD)
+            if step < 2:
+                we_q.append(quantise(we_raw[step], f"we{step}", 4, False, f"we{step}_w"))
+            if SP == 1:
+                some_scores(step)

@@ -19,31 +19,21 @@ ALU = mybir.AluOpType
 
 P = 128
 PACK = 4
-PASSES = K // (P * PACK)
+K_PASS = P * PACK
+PASSES = K // K_PASS
 QUADS = 4
-CHUNK = 256
-CHUNKS = S // CHUNK
+BANK = 512
 UNIT = 128
 UNITS = S // UNIT
-ZB = 1
-AB = 1
-BB = 1
-HB = 1
-YB = 4
-AHEAD = 1
-PF = 1
-SP = 1
-LAG = 2
-PER_STEP = 2
-FINE = 3
-VS = 6
-BANK = 512
-HOLD = {}
-FIRST = [(0, 1)]
-EVEN = [(1, 1)]
-ODD = [(2, 1), (0, 2)]
+CHUNK = 2 * UNIT
+CHUNKS = S // CHUNK
+PER_COLUMN = 16
 N_TILES = N // P
-HALF = N // 2
+WIDTH = 512
+LAST, PREV, OLDER = 0, 1, 2
+WE_PIECES = 4
+FIRST_SCORES = 2
+BANKS_A_STEP = 2
 
 
 def tile_list_session_gate_scores_kernel(
@@ -52,10 +42,10 @@ def tile_list_session_gate_scores_kernel(
     nc = tc.nc
     with ExitStack() as ctx:
         keep = ctx.enter_context(tc.tile_pool(name="keep", bufs=1))
-        ring = ctx.enter_context(tc.tile_pool(name="ring", bufs=2))
+        ring = ctx.enter_context(tc.tile_pool(name="ring", bufs=8))
         psum = ctx.enter_context(tc.psum_pool(name="psum", bufs=1))
 
-        lists = [keep.tile([P, S // 16], U16, name=f"list{i}") for i in range(3)]
+        lists = [keep.tile([P, S // PER_COLUMN], U16, name=f"list{i}") for i in range(3)]
         tab_s = keep.tile([P, T], U8, tag="tab_s", align_bytes=64)
         tab_w = [keep.tile([P, T], I32, name=f"tab_w{a}", align_bytes=64) for a in range(PASSES)]
         wg_w = keep.tile([P, PASSES, 2 * H], U8, align_bytes=64)
@@ -65,19 +55,22 @@ def tile_list_session_gate_scores_kernel(
         last_s1 = keep.tile([P, S], U8, align_bytes=64)
         bias = keep.tile([P, N_TILES], F32)
         ident = keep.tile([P, P], F32)
-        warm = keep.tile([P, 2], F32)
 
         nc.vector.memset(tab_s[:].bitcast(I32), 0)
         nc.vector.memset(wg_s[:].bitcast(I32), 0)
         nc.vector.memset(wo_s[:].bitcast(I32), 0)
         nc.vector.memset(last_s1[:].bitcast(I32), 0)
-        nc.vector.memset(warm[:, 0:1], 0.0)
         nc.vector.memset(ident[:], 0.0)
-        nc.scalar.activation(warm[:, 1:2], warm[:, 0:1], ACT.Sigmoid)
+        minus_one = [
+            keep.tile([P, 1], F32, name=f"minus_one{u}", tag=f"minus_one{u}", align_bytes=64) for u in range(UNITS)
+        ]
+        for column in minus_one:
+            nc.vector.memset(column[:], -1.0)
+
         for q in range(QUADS):
             nc.gpsimd.dma_start(
                 wg_s[32 * q : 32 * q + 4, :, :].bitcast(I32),
-                wg_scales[:, 4 * q : 4 * q + 4, :].rearrange("a r c -> r a c").bitcast(I32),
+                wg_scales[:, 4 * q : 4 * q + 4, :].rearrange("a i c -> i a c").bitcast(I32),
             )
         for q in range(QUADS):
             nc.gpsimd.dma_start(
@@ -85,245 +78,187 @@ def tile_list_session_gate_scores_kernel(
             )
         make_identity(nc, ident[:], nomemset=True)
 
-        nc.sync.dma_start(lists[0][:], offs)
+        nc.sync.dma_start(lists[LAST][:], offs)
         for q in range(QUADS):
             nc.sync.dma_start(
                 tab_s[32 * q : 32 * q + 8, :].bitcast(I32), tab_scales[:, 4 * q : 4 * q + 4, :].bitcast(I32)
             )
 
         got_s = [keep.tile([P, S], U8, name=f"got_s{i}", align_bytes=64) for i in range(3)]
-        nc.vector.tensor_copy(got_s[0][:], tab_s[:].indirect(lists[0][:]))
+        nc.vector.tensor_copy(got_s[LAST][:], tab_s[:].indirect(lists[LAST][:]))
 
         def load_rows(rows, name, tag):
-            raw = keep.tile([P, PACK, HALF], F32, name=name, tag=tag, align_bytes=64)
-            nc.sync.dma_start(raw[:], rows.rearrange("(p j) w -> p j w", j=PACK))
+            raw = keep.tile([P, PACK, WIDTH], F32, name=name, tag=tag, align_bytes=64)
+            nc.sync.dma_start(raw[:], rows.rearrange("(p t) w -> p t w", t=PACK))
             return raw
 
-        def load_dealt(rows, name, tag):
-            raw = keep.tile([P, PACK, HALF], F32, name=name, tag=tag, align_bytes=64)
-            by_slot = rows.rearrange("(q t i) w -> t q i w", t=PACK, i=8)
-            for t in range(PACK):
-                nc.sync.dma_start(raw[:, t, :], by_slot[t])
-            return raw
-
-        def quantise(raw, name, pieces, dealt, tag):
-            grouped = keep.tile([P, HALF, PACK], BF16, name=name + "_b", tag=name + "_b", align_bytes=64)
+        def quantise(raw, name, pieces):
+            grouped = keep.tile([P, WIDTH, PACK], BF16, name=name + "_b", tag=name + "_b", align_bytes=64)
             for k in range(pieces):
-                part = slice(k * HALF // pieces, (k + 1) * HALF // pieces)
-                if dealt:
-                    nc.scalar.activation(
-                        grouped[:, part, :].rearrange("p (q i) j -> p q i j", i=8),
-                        raw[:].rearrange("p j (q t i) -> p t q i j", t=PACK, i=8)[:, k],
-                        ACT.Copy,
-                        scale=-1.0,
-                    )
-                else:
-                    nc.scalar.copy(
-                        grouped[:, part, :].rearrange("p (c i) t -> p c t i", i=4),
-                        raw[:, :, part].rearrange("p t (c i) -> p c t i", i=4),
-                    )
-            codes = keep.tile([P, HALF], U32, name=name + "_w", tag=tag, align_bytes=64)
-            scales = keep.tile([P, HALF], U8, name=name + "_s", align_bytes=64)
+                part = slice(k * WIDTH // pieces, (k + 1) * WIDTH // pieces)
+                nc.scalar.copy(
+                    grouped[:, part, :].rearrange("p (c i) t -> p c t i", i=4),
+                    raw[:, :, part].rearrange("p t (c i) -> p c t i", i=4),
+                )
+            codes = keep.tile([P, WIDTH], U32, name=name + "_w", align_bytes=64)
+            scales = keep.tile([P, WIDTH], U8, name=name + "_s", align_bytes=64)
             nc.vector.quantize_mx(codes[:].bitcast(FP8X4), scales[:], grouped[:].rearrange("p c t -> p (c t)"))
             return codes, scales
 
         def load_table(a):
-            nc.sync.dma_start(tab_w[a][:], tab_words[a].rearrange("p t i -> p (t i)").bitcast(I32))
+            nc.sync.dma_start(tab_w[a][:], tab_words[a].rearrange("p c t -> p (c t)").bitcast(I32))
 
-        nc.sync.dma_start(lists[1][:], offs2)
-        nc.sync.dma_start(lists[2][:], offs3)
-        wp_raw = [load_rows(wp[0:512, :], "wp0", "wp0")]
-        for i in (1, 2):
+        nc.sync.dma_start(lists[PREV][:], offs2)
+        nc.sync.dma_start(lists[OLDER][:], offs3)
+        wp_raw = [load_rows(wp[0:K_PASS, :], "wp0", "wp0")]
+        for i in (PREV, OLDER):
             nc.vector.tensor_copy(got_s[i][:], tab_s[:].indirect(lists[i][:]))
         load_table(0)
         nc.sync.dma_start(wg_w[:].bitcast(I32), wg_words.rearrange("a p c -> p a c").bitcast(I32))
-        wp_raw.append(load_rows(wp[512:1024, :], "wp1", "wp1"))
+        wp_raw.append(load_rows(wp[K_PASS:K, :], "wp1", "wp1"))
         for q in range(QUADS):
             nc.scalar.dma_start(
-                last_s1[32 * q : 32 * q + 4, :].bitcast(I32), got_s[0][32 * q + 4 : 32 * q + 8, :].bitcast(I32)
+                last_s1[32 * q : 32 * q + 4, :].bitcast(I32), got_s[LAST][32 * q + 4 : 32 * q + 8, :].bitcast(I32)
             )
         load_table(1)
-        nc.sync.dma_start(wo_w[:], wo_words.rearrange("a p c i -> p a (c i)").bitcast(I32))
-        wp_q = [quantise(wp_raw[a], f"wp{a}", PACK, True, f"wp{a}_w") for a in range(PASSES)]
+        nc.sync.dma_start(wo_w[:], wo_words.rearrange("a p c t -> p a (c t)").bitcast(I32))
+        wp_q = [quantise(wp_raw[a], f"wp{a}", 1) for a in range(PASSES)]
         we_raw = [
-            load_dealt(we[:, h * HALF : (h + 1) * HALF], f"we{h}", tag) for h, tag in enumerate(("tab_s", "wp0"))
+            load_rows(we[:, half * WIDTH : (half + 1) * WIDTH], f"we{half}", tag)
+            for half, tag in enumerate(("tab_s", "wp0"))
         ]
-
-        we_q = []
-
         with nc.allow_non_contiguous_dma(reason="one bias value a partition and output tile"):
-            nc.sync.dma_start(bias[:], be.rearrange("(t p) -> p t", p=P))
-        out_v = out.rearrange("(t p) j -> p t j", p=P)
-        got = {}
+            nc.sync.dma_start(bias[:], be.rearrange("(m p) -> p m", p=P))
 
-        def gather(i, c, a, dest):
-            got[i, c, a] = dest
-            cols = slice(c * CHUNK // 16, (c + 1) * CHUNK // 16)
-            nc.vector.tensor_copy(dest, tab_w[a][:].bitcast(U32).indirect(lists[i][:, cols]))
+        out_tiles = out.rearrange("(m p) j -> p m j", p=P)
+        dealt = "j (p t) -> j t p"
+        got_w, gates, sums, terms, states = {}, {}, {}, {}, {}
+        we_q, waiting = [], []
 
-        def gather_into(tag, wanted):
-            wanted = [(i, c) for i, c in wanted if c < CHUNKS]
-            if wanted:
-                dest = keep.tile([P, len(wanted), PASSES, CHUNK], U32, name="got_" + tag, tag=tag, align_bytes=64)
-                for k, (i, c) in enumerate(wanted):
-                    for a in range(PASSES):
-                        gather(i, c, a, dest[:, k, a, :])
+        def gather_words(i, c, a, dest):
+            got_w[i, c, a] = dest
+            entries = lists[i][:, c * CHUNK // PER_COLUMN : (c + 1) * CHUNK // PER_COLUMN]
+            nc.vector.tensor_copy(dest, tab_w[a][:].bitcast(U32).indirect(entries))
 
-        first = keep.tile([P, PASSES, 3, CHUNK], U32, align_bytes=64)
-        for a in range(PASSES):
-            for i in range(3):
-                gather(i, 0, a, first[:, a, i, :])
-        gather_into("wp1_b", FIRST)
+        def gather_behind(tag, which, c):
+            dest = keep.tile([P, len(which), PASSES, CHUNK], U32, name="got_" + tag, tag=tag, align_bytes=64)
+            for k, i in enumerate(which):
+                for a in range(PASSES):
+                    gather_words(i, c, a, dest[:, k, a, :])
 
-        dealt = "j (q t i) -> j t q i"
-        by_block = "j t (q i) -> j t q i"
-        sums = {}
-        terms = {}
-        states = {}
-        waiting = []
+        def product(acc, i, u, table_scales, weights):
+            c, v = divmod(u, 2)
+            for a in range(PASSES):
+                nc.tensor.matmul_mx(
+                    acc[:],
+                    lhsT=got_w[i, c, a][:, v * UNIT : (v + 1) * UNIT].bitcast(FP8X4),
+                    lhsT_scale=table_scales[a][:, u * UNIT : (u + 1) * UNIT],
+                    rhs=weights[a][0],
+                    rhs_scale=weights[a][1],
+                    start=(a == 0),
+                    stop=(a == PASSES - 1),
+                )
 
-        gates = {}
+        wg_mx = [(wg_w[:, a, :].bitcast(FP4X4), wg_s[:, a, :]) for a in range(PASSES)]
+        wp_mx = [(codes[:].bitcast(FP8X4), scales[:]) for codes, scales in wp_q]
+        wo_mx = [(wo_w[:, a, :].bitcast(FP8X4), wo_s[4 * a :, :]) for a in range(PASSES)]
 
         def gate_of(u):
-            c, v = divmod(u, 2)
-            loc = slice(v * UNIT, (v + 1) * UNIT)
-            glob = slice(u * UNIT, (u + 1) * UNIT)
-            z_ps = psum.tile([P, H], F32, bufs=ZB)
-            for a in range(PASSES):
-                nc.tensor.matmul_mx(
-                    z_ps[:],
-                    lhsT=got[0, c, a][:, loc].bitcast(FP8X4),
-                    lhsT_scale=(got_s[0] if a == 0 else last_s1)[:, glob],
-                    rhs=wg_w[:, a, :].bitcast(FP4X4),
-                    rhs_scale=wg_s[:, a, :],
-                    start=(a == 0),
-                    stop=(a == PASSES - 1),
-                )
-            gate = keep.tile([P, PACK, P], F32, name="gate", tag=f"gate{u}", align_bytes=64)
-            nc.scalar.activation(
-                gate[:].rearrange(by_block, i=8), z_ps[:].rearrange(dealt, t=PACK, i=8), ACT.Sigmoid, scale=-1.0
-            )
-            gates[u] = gate
+            z_ps = psum.tile([P, H], F32)
+            product(z_ps, LAST, u, [got_s[LAST][:], last_s1[:]], wg_mx)
+            gates[u] = keep.tile([P, PACK, P], F32, name=f"gate{u}", align_bytes=64)
+            nc.scalar.activation(gates[u][:], z_ps[:].rearrange(dealt, t=PACK), ACT.Sigmoid)
 
         def products(u):
-            c, v = divmod(u, 2)
-            loc = slice(v * UNIT, (v + 1) * UNIT)
-            glob = slice(u * UNIT, (u + 1) * UNIT)
-            a_ps = psum.tile([P, H], F32, bufs=AB)
-            b_ps = psum.tile([P, H], F32, bufs=BB)
-            for a in range(PASSES):
-                nc.tensor.matmul_mx(
-                    a_ps[:],
-                    lhsT=got[1, c, a][:, loc].bitcast(FP8X4),
-                    lhsT_scale=got_s[1][4 * a :, glob],
-                    rhs=wp_q[a][0][:].bitcast(FP8X4),
-                    rhs_scale=wp_q[a][1][:],
-                    start=(a == 0),
-                    stop=(a == PASSES - 1),
-                )
-            for a in range(PASSES):
-                nc.tensor.matmul_mx(
-                    b_ps[:],
-                    lhsT=got[2, c, a][:, loc].bitcast(FP8X4),
-                    lhsT_scale=got_s[2][4 * a :, glob],
-                    rhs=wo_w[:, a, :].bitcast(FP8X4),
-                    rhs_scale=wo_s[4 * a :, :],
-                    start=(a == 0),
-                    stop=(a == PASSES - 1),
-                )
+            a_ps = psum.tile([P, H], F32, bufs=2)
+            b_ps = psum.tile([P, H], F32, bufs=2)
+            product(a_ps, PREV, u, [got_s[PREV][4 * a :, :] for a in range(PASSES)], wp_mx)
+            product(b_ps, OLDER, u, [got_s[OLDER][4 * a :, :] for a in range(PASSES)], wo_mx)
             sums[u] = (a_ps, b_ps)
 
         def gated_terms(u):
-            c, v = divmod(u, 2)
-            gate = gates[u]
             a_ps, b_ps = sums[u]
-            both = keep.tile([P, 2, PACK, P], F32, name="terms", tag=HOLD.get(u, f"terms{u}"), align_bytes=64)
-            neg_ga = both[:, 0]
-            neg_rest = both[:, 1]
+            terms[u] = keep.tile([P, 2, PACK, P], F32, name=f"terms{u}", align_bytes=64)
             nc.vector.scalar_tensor_tensor(
-                neg_ga[:], gate[:], 1.0, a_ps[:].rearrange("j (t p) -> j t p", t=PACK), ALU.subtract, ALU.mult
+                terms[u][:, 0], gates[u][:], minus_one[u][:], a_ps[:].rearrange(dealt, t=PACK), ALU.mult, ALU.mult
             )
-            nc.vector.tensor_tensor(
-                neg_rest[:].rearrange(by_block, i=8),
-                gate[:].rearrange(by_block, i=8),
-                b_ps[:].rearrange(dealt, t=PACK, i=8),
-                ALU.mult,
+            nc.vector.scalar_tensor_tensor(
+                terms[u][:, 1], gates[u][:], 1.0, b_ps[:].rearrange(dealt, t=PACK), ALU.subtract, ALU.mult
             )
-            terms[u] = (neg_ga, neg_rest)
-            gather_into(f"gate{u}", [(i, c + k) for i, k in (EVEN if v == 0 else ODD)])
+            c, v = divmod(u, 2)
+            if v == 0 and c + 1 < CHUNKS:
+                gather_behind(f"minus_one{u}", (PREV, OLDER), c + 1)
+            if v == 1 and c + 2 < CHUNKS:
+                gather_behind(f"minus_one{u}", (LAST,), c + 2)
 
         def turn(u):
             c, v = divmod(u, 2)
-            neg_ga, neg_rest = terms[u]
             if v == 0:
-                states[c] = keep.tile([P, CHUNK, PACK], BF16, name="state", tag=f"state{c}", align_bytes=64)
-            h_ps = psum.tile([P, PACK, UNIT], F32, bufs=HB)
+                states[c] = keep.tile([P, CHUNK, PACK], BF16, name=f"state{c}", align_bytes=64)
+            h_ps = psum.tile([P, PACK, UNIT], F32)
             for t in range(PACK):
-                nc.tensor.matmul(h_ps[:, t, :], neg_rest[:, t, :], ident[:], start=True, stop=False, is_transpose=True)
-                nc.tensor.matmul(h_ps[:, t, :], neg_ga[:, t, :], ident[:], start=False, stop=True, is_transpose=True)
-            nc.scalar.copy(states[c][:, v * UNIT : (v + 1) * UNIT, :], h_ps[:].rearrange("p t j -> p j t"))
-            if c >= FINE:
-                pack(u * UNIT, UNIT, states[c][:, v * UNIT : (v + 1) * UNIT, :])
+                nc.tensor.matmul(h_ps[:, t, :], terms[u][:, 1, t, :], ident[:], start=True, stop=False, is_transpose=True)
+                nc.tensor.matmul(h_ps[:, t, :], terms[u][:, 0, t, :], ident[:], start=False, stop=True, is_transpose=True)
+            mine = states[c][:, v * UNIT : (v + 1) * UNIT, :]
+            nc.scalar.activation(mine, h_ps[:].rearrange("p t j -> p j t"), ACT.Copy, scale=-1.0)
+            if c == CHUNKS - 1:
+                pack_state(u * UNIT, UNIT, mine)
             elif v == 1:
-                pack(c * CHUNK, CHUNK, states[c][:])
+                pack_state(c * CHUNK, CHUNK, states[c][:])
 
-        def pack(j0, width, values):
-            h_w = keep.tile([P, width], U32, name=f"h_w{j0}", align_bytes=64)
-            h_s = keep.tile([P, width], U8, name=f"h_s{j0}", align_bytes=64)
+        def pack_state(j0, sessions, values):
+            h_w = keep.tile([P, sessions], U32, name=f"h_w{j0}", align_bytes=64)
+            h_s = keep.tile([P, sessions], U8, name=f"h_s{j0}", align_bytes=64)
             nc.vector.quantize_mx(h_w[:].bitcast(FP8X4), h_s[:], values.rearrange("p j t -> p (j t)"))
-            per_bank = BANK // width
-            for first_tile in range(0, N_TILES, per_bank):
-                waiting.append((h_w, h_s, j0, width, first_tile))
+            for first_tile in range(0, N_TILES, BANK // sessions):
+                waiting.append((h_w, h_s, j0, sessions, first_tile))
 
-        def scores(on_vector):
-            h_w, h_s, j0, width, first_tile = waiting.pop(0)
-            per_bank = BANK // width
-            y_ps = psum.tile([P, per_bank, width], F32, bufs=YB)
-            y_sb = ring.tile([P, per_bank, width], F32, bufs=8)
-            for e in range(per_bank):
-                nt = first_tile + e
-                codes, scales = we_q[nt * P // HALF]
-                ncols = slice(nt * P % HALF, nt * P % HALF + P)
+        def scores(on_vector, tag, bufs):
+            h_w, h_s, j0, sessions, first_tile = waiting.pop(0)
+            tiles = range(first_tile, first_tile + BANK // sessions)
+            y_ps = psum.tile([P, len(tiles), sessions], F32, tag=tag, bufs=bufs)
+            y_sb = ring.tile([P, len(tiles), sessions], F32)
+            for e, m in enumerate(tiles):
+                codes, scales = we_q[m * P // WIDTH]
+                columns = slice(m * P % WIDTH, m * P % WIDTH + P)
                 nc.tensor.matmul_mx(
                     y_ps[:, e, :],
-                    lhsT=codes[:, ncols].bitcast(FP8X4),
-                    lhsT_scale=scales[:, ncols],
+                    lhsT=codes[:, columns].bitcast(FP8X4),
+                    lhsT_scale=scales[:, columns],
                     rhs=h_w[:].bitcast(FP8X4),
                     rhs_scale=h_s[:],
                     start=True,
                     stop=True,
                 )
-            for e in range(per_bank):
-                nt = first_tile + e
+            for e, m in enumerate(tiles):
                 if on_vector:
-                    nc.vector.tensor_scalar_add(y_sb[:, e, :], y_ps[:, e, :], bias[:, nt : nt + 1])
+                    nc.vector.tensor_scalar_add(y_sb[:, e, :], y_ps[:, e, :], bias[:, m : m + 1])
                 else:
-                    nc.scalar.activation(y_sb[:, e, :], y_ps[:, e, :], ACT.Identity, bias=bias[:, nt : nt + 1])
-            nc.sync.dma_start(out_v[:, first_tile : first_tile + per_bank, j0 : j0 + width], y_sb[:])
+                    nc.scalar.activation(y_sb[:, e, :], y_ps[:, e, :], ACT.Identity, bias=bias[:, m : m + 1])
+            nc.sync.dma_start(out_tiles[:, first_tile : first_tile + len(tiles), j0 : j0 + sessions], y_sb[:])
 
-        def some_scores(step):
-            if step >= LAG:
-                for k in range(min(PER_STEP if step < UNITS else len(waiting), len(waiting))):
-                    scores(step >= VS and k % 2 == 1)
+        first = keep.tile([P, PASSES, 3, CHUNK], U32, align_bytes=64)
+        for a in range(PASSES):
+            for i in (LAST, PREV, OLDER):
+                gather_words(i, 0, a, first[:, a, i, :])
+        gather_behind("wp1_b", (LAST,), 1)
 
         gate_of(0)
-        for u in range(AHEAD):
-            products(u)
+        products(0)
+        products(1)
         gate_of(1)
-        for step in range(UNITS + 1):
-            if step < UNITS:
-                gated_terms(step)
-            if PF and step + AHEAD < UNITS:
-                products(step + AHEAD)
-            if SP == 0:
-                some_scores(step)
-            if step < UNITS:
-                turn(step)
+        for step in range(UNITS):
+            gated_terms(step)
+            turn(step)
             if step + 2 < UNITS:
                 gate_of(step + 2)
-            if not PF and step + AHEAD < UNITS:
-                products(step + AHEAD)
-            if step < 2:
-                we_q.append(quantise(we_raw[step], f"we{step}", 4, False, f"we{step}_w"))
-            if SP == 1:
-                some_scores(step)
+                products(step + 2)
+            if step < N // WIDTH:
+                we_q.append(quantise(we_raw[step], f"we{step}", WE_PIECES))
+            if FIRST_SCORES <= step < UNITS - 2:
+                for bank in range(BANKS_A_STEP):
+                    scores(False, "y_ps", 2)
+
+        banks = [("y_ps", 2), ("y_ps", 2), ("z_ps", 1), ("a_ps", 2), ("a_ps", 2), ("b_ps", 2), ("b_ps", 2)]
+        for k in range(len(waiting)):
+            scores(k % 2 == 1, *banks[k % len(banks)])

from contextlib import ExitStack

import concourse.mybir as mybir
from concourse.masks import make_identity

K, H, N, T, S = 1024, 512, 1024, 2048, 1024
FLOPS = 2 * (3 * K * H * S + H * N * S)

F32 = mybir.dt.float32
BF16 = mybir.dt.bfloat16
I32 = mybir.dt.int32
U32 = mybir.dt.uint32
U16 = mybir.dt.uint16
U8 = mybir.dt.uint8
FP8X4 = mybir.dt.float8_e4m3fn_x4
FP4X4 = mybir.dt.float4_e2m1fn_x4
ACT = mybir.ActivationFunctionType
ALU = mybir.AluOpType

P = 128
PACK = 4
K_PASS = P * PACK
PASSES = K // K_PASS
QUADS = 4
BANK = 512
UNIT = 128
UNITS = S // UNIT
CHUNK = 2 * UNIT
CHUNKS = S // CHUNK
PER_COLUMN = 16
N_TILES = N // P
WIDTH = 512
LAST, PREV, OLDER = 0, 1, 2
WE_PIECES = 4
FIRST_SCORES = 2
BANKS_A_STEP = 2


def tile_list_session_gate_scores_kernel(
    tc, tab_words, tab_scales, offs, offs2, offs3, wg_words, wg_scales, wp, wo_words, wo_scales, we, be, out
):
    nc = tc.nc
    with ExitStack() as ctx:
        keep = ctx.enter_context(tc.tile_pool(name="keep", bufs=1))
        ring = ctx.enter_context(tc.tile_pool(name="ring", bufs=8))
        psum = ctx.enter_context(tc.psum_pool(name="psum", bufs=1))

        lists = [keep.tile([P, S // PER_COLUMN], U16, name=f"list{i}") for i in range(3)]
        tab_s = keep.tile([P, T], U8, tag="tab_s", align_bytes=64)
        tab_w = [keep.tile([P, T], I32, name=f"tab_w{a}", align_bytes=64) for a in range(PASSES)]
        wg_w = keep.tile([P, PASSES, 2 * H], U8, align_bytes=64)
        wg_s = keep.tile([P, PASSES, H], U8, align_bytes=64)
        wo_w = keep.tile([P, PASSES, H], I32, align_bytes=64)
        wo_s = keep.tile([P, H], U8, align_bytes=64)
        last_s1 = keep.tile([P, S], U8, align_bytes=64)
        bias = keep.tile([P, N_TILES], F32)
        ident = keep.tile([P, P], F32)

        nc.vector.memset(tab_s[:].bitcast(I32), 0)
        nc.vector.memset(wg_s[:].bitcast(I32), 0)
        nc.vector.memset(wo_s[:].bitcast(I32), 0)
        nc.vector.memset(last_s1[:].bitcast(I32), 0)
        nc.vector.memset(ident[:], 0.0)
        minus_one = [
            keep.tile([P, 1], F32, name=f"minus_one{u}", tag=f"minus_one{u}", align_bytes=64) for u in range(UNITS)
        ]
        for column in minus_one:
            nc.vector.memset(column[:], -1.0)

        for q in range(QUADS):
            nc.gpsimd.dma_start(
                wg_s[32 * q : 32 * q + 4, :, :].bitcast(I32),
                wg_scales[:, 4 * q : 4 * q + 4, :].rearrange("a i c -> i a c").bitcast(I32),
            )
        for q in range(QUADS):
            nc.gpsimd.dma_start(
                wo_s[32 * q : 32 * q + 8, :].bitcast(I32), wo_scales[:, 4 * q : 4 * q + 4, :].bitcast(I32)
            )
        make_identity(nc, ident[:], nomemset=True)

        nc.sync.dma_start(lists[LAST][:], offs)
        for q in range(QUADS):
            nc.sync.dma_start(
                tab_s[32 * q : 32 * q + 8, :].bitcast(I32), tab_scales[:, 4 * q : 4 * q + 4, :].bitcast(I32)
            )

        got_s = [keep.tile([P, S], U8, name=f"got_s{i}", align_bytes=64) for i in range(3)]
        nc.vector.tensor_copy(got_s[LAST][:], tab_s[:].indirect(lists[LAST][:]))

        def load_rows(rows, name, tag):
            raw = keep.tile([P, PACK, WIDTH], F32, name=name, tag=tag, align_bytes=64)
            nc.sync.dma_start(raw[:], rows.rearrange("(p t) w -> p t w", t=PACK))
            return raw

        def quantise(raw, name, pieces):
            grouped = keep.tile([P, WIDTH, PACK], BF16, name=name + "_b", tag=name + "_b", align_bytes=64)
            for k in range(pieces):
                part = slice(k * WIDTH // pieces, (k + 1) * WIDTH // pieces)
                nc.scalar.copy(
                    grouped[:, part, :].rearrange("p (c i) t -> p c t i", i=4),
                    raw[:, :, part].rearrange("p t (c i) -> p c t i", i=4),
                )
            codes = keep.tile([P, WIDTH], U32, name=name + "_w", align_bytes=64)
            scales = keep.tile([P, WIDTH], U8, name=name + "_s", align_bytes=64)
            nc.vector.quantize_mx(codes[:].bitcast(FP8X4), scales[:], grouped[:].rearrange("p c t -> p (c t)"))
            return codes, scales

        def load_table(a):
            nc.sync.dma_start(tab_w[a][:], tab_words[a].rearrange("p c t -> p (c t)").bitcast(I32))

        nc.sync.dma_start(lists[PREV][:], offs2)
        nc.sync.dma_start(lists[OLDER][:], offs3)
        wp_raw = [load_rows(wp[0:K_PASS, :], "wp0", "wp0")]
        for i in (PREV, OLDER):
            nc.vector.tensor_copy(got_s[i][:], tab_s[:].indirect(lists[i][:]))
        load_table(0)
        nc.sync.dma_start(wg_w[:].bitcast(I32), wg_words.rearrange("a p c -> p a c").bitcast(I32))
        wp_raw.append(load_rows(wp[K_PASS:K, :], "wp1", "wp1"))
        for q in range(QUADS):
            nc.scalar.dma_start(
                last_s1[32 * q : 32 * q + 4, :].bitcast(I32), got_s[LAST][32 * q + 4 : 32 * q + 8, :].bitcast(I32)
            )
        load_table(1)
        nc.sync.dma_start(wo_w[:], wo_words.rearrange("a p c t -> p a (c t)").bitcast(I32))
        wp_q = [quantise(wp_raw[a], f"wp{a}", 1) for a in range(PASSES)]
        we_raw = [
            load_rows(we[:, half * WIDTH : (half + 1) * WIDTH], f"we{half}", tag)
            for half, tag in enumerate(("tab_s", "wp0"))
        ]
        with nc.allow_non_contiguous_dma(reason="one bias value a partition and output tile"):
            nc.sync.dma_start(bias[:], be.rearrange("(m p) -> p m", p=P))

        out_tiles = out.rearrange("(m p) j -> p m j", p=P)
        dealt = "j (p t) -> j t p"
        got_w, gates, sums, terms, states = {}, {}, {}, {}, {}
        we_q, waiting = [], []

        def gather_words(i, c, a, dest):
            got_w[i, c, a] = dest
            entries = lists[i][:, c * CHUNK // PER_COLUMN : (c + 1) * CHUNK // PER_COLUMN]
            nc.vector.tensor_copy(dest, tab_w[a][:].bitcast(U32).indirect(entries))

        def gather_behind(tag, which, c):
            dest = keep.tile([P, len(which), PASSES, CHUNK], U32, name="got_" + tag, tag=tag, align_bytes=64)
            for k, i in enumerate(which):
                for a in range(PASSES):
                    gather_words(i, c, a, dest[:, k, a, :])

        def product(acc, i, u, table_scales, weights):
            c, v = divmod(u, 2)
            for a in range(PASSES):
                nc.tensor.matmul_mx(
                    acc[:],
                    lhsT=got_w[i, c, a][:, v * UNIT : (v + 1) * UNIT].bitcast(FP8X4),
                    lhsT_scale=table_scales[a][:, u * UNIT : (u + 1) * UNIT],
                    rhs=weights[a][0],
                    rhs_scale=weights[a][1],
                    start=(a == 0),
                    stop=(a == PASSES - 1),
                )

        wg_mx = [(wg_w[:, a, :].bitcast(FP4X4), wg_s[:, a, :]) for a in range(PASSES)]
        wp_mx = [(codes[:].bitcast(FP8X4), scales[:]) for codes, scales in wp_q]
        wo_mx = [(wo_w[:, a, :].bitcast(FP8X4), wo_s[4 * a :, :]) for a in range(PASSES)]

        def gate_of(u):
            z_ps = psum.tile([P, H], F32)
            product(z_ps, LAST, u, [got_s[LAST][:], last_s1[:]], wg_mx)
            gates[u] = keep.tile([P, PACK, P], F32, name=f"gate{u}", align_bytes=64)
            nc.scalar.activation(gates[u][:], z_ps[:].rearrange(dealt, t=PACK), ACT.Sigmoid)

        def products(u):
            a_ps = psum.tile([P, H], F32, bufs=2)
            b_ps = psum.tile([P, H], F32, bufs=2)
            product(a_ps, PREV, u, [got_s[PREV][4 * a :, :] for a in range(PASSES)], wp_mx)
            product(b_ps, OLDER, u, [got_s[OLDER][4 * a :, :] for a in range(PASSES)], wo_mx)
            sums[u] = (a_ps, b_ps)

        def gated_terms(u):
            a_ps, b_ps = sums[u]
            terms[u] = keep.tile([P, 2, PACK, P], F32, name=f"terms{u}", align_bytes=64)
            nc.vector.scalar_tensor_tensor(
                terms[u][:, 0], gates[u][:], minus_one[u][:], a_ps[:].rearrange(dealt, t=PACK), ALU.mult, ALU.mult
            )
            nc.vector.scalar_tensor_tensor(
                terms[u][:, 1], gates[u][:], 1.0, b_ps[:].rearrange(dealt, t=PACK), ALU.subtract, ALU.mult
            )
            c, v = divmod(u, 2)
            if v == 0 and c + 1 < CHUNKS:
                gather_behind(f"minus_one{u}", (PREV, OLDER), c + 1)
            if v == 1 and c + 2 < CHUNKS:
                gather_behind(f"minus_one{u}", (LAST,), c + 2)

        def turn(u):
            c, v = divmod(u, 2)
            if v == 0:
                states[c] = keep.tile([P, CHUNK, PACK], BF16, name=f"state{c}", align_bytes=64)
            h_ps = psum.tile([P, PACK, UNIT], F32)
            for t in range(PACK):
                nc.tensor.matmul(h_ps[:, t, :], terms[u][:, 1, t, :], ident[:], start=True, stop=False, is_transpose=True)
                nc.tensor.matmul(h_ps[:, t, :], terms[u][:, 0, t, :], ident[:], start=False, stop=True, is_transpose=True)
            mine = states[c][:, v * UNIT : (v + 1) * UNIT, :]
            nc.scalar.activation(mine, h_ps[:].rearrange("p t j -> p j t"), ACT.Copy, scale=-1.0)
            if c == CHUNKS - 1:
                pack_state(u * UNIT, UNIT, mine)
            elif v == 1:
                pack_state(c * CHUNK, CHUNK, states[c][:])

        def pack_state(j0, sessions, values):
            h_w = keep.tile([P, sessions], U32, name=f"h_w{j0}", align_bytes=64)
            h_s = keep.tile([P, sessions], U8, name=f"h_s{j0}", align_bytes=64)
            nc.vector.quantize_mx(h_w[:].bitcast(FP8X4), h_s[:], values.rearrange("p j t -> p (j t)"))
            for first_tile in range(0, N_TILES, BANK // sessions):
                waiting.append((h_w, h_s, j0, sessions, first_tile))

        def scores(on_vector, tag, bufs):
            h_w, h_s, j0, sessions, first_tile = waiting.pop(0)
            tiles = range(first_tile, first_tile + BANK // sessions)
            y_ps = psum.tile([P, len(tiles), sessions], F32, tag=tag, bufs=bufs)
            y_sb = ring.tile([P, len(tiles), sessions], F32)
            for e, m in enumerate(tiles):
                codes, scales = we_q[m * P // WIDTH]
                columns = slice(m * P % WIDTH, m * P % WIDTH + P)
                nc.tensor.matmul_mx(
                    y_ps[:, e, :],
                    lhsT=codes[:, columns].bitcast(FP8X4),
                    lhsT_scale=scales[:, columns],
                    rhs=h_w[:].bitcast(FP8X4),
                    rhs_scale=h_s[:],
                    start=True,
                    stop=True,
                )
            for e, m in enumerate(tiles):
                if on_vector:
                    nc.vector.tensor_scalar_add(y_sb[:, e, :], y_ps[:, e, :], bias[:, m : m + 1])
                else:
                    nc.scalar.activation(y_sb[:, e, :], y_ps[:, e, :], ACT.Identity, bias=bias[:, m : m + 1])
            nc.sync.dma_start(out_tiles[:, first_tile : first_tile + len(tiles), j0 : j0 + sessions], y_sb[:])

        first = keep.tile([P, PASSES, 3, CHUNK], U32, align_bytes=64)
        for a in range(PASSES):
            for i in (LAST, PREV, OLDER):
                gather_words(i, 0, a, first[:, a, i, :])
        gather_behind("wp1_b", (LAST,), 1)

        gate_of(0)
        products(0)
        products(1)
        gate_of(1)
        for step in range(UNITS):
            gated_terms(step)
            turn(step)
            if step + 2 < UNITS:
                gate_of(step + 2)
                products(step + 2)
            if step < N // WIDTH:
                we_q.append(quantise(we_raw[step], f"we{step}", WE_PIECES))
            if FIRST_SCORES <= step < UNITS - 2:
                for bank in range(BANKS_A_STEP):
                    scores(False, "y_ps", 2)

        banks = [("y_ps", 2), ("y_ps", 2), ("z_ps", 1), ("a_ps", 2), ("a_ps", 2), ("b_ps", 2), ("b_ps", 2)]
        for k in range(len(waiting)):
            scores(k % 2 == 1, *banks[k % len(banks)])
